import numpy as np
import ml_dtypes


def mxq(x, axis, fmt="e4m3"):
    dtype, down = {"e4m3": (ml_dtypes.float8_e4m3fn, 7), "e5m2": (ml_dtypes.float8_e5m2, 14)}[fmt]
    v = np.moveaxis(np.asarray(x, np.float32).astype(ml_dtypes.bfloat16).astype(np.float64), axis, -1)
    blocks = v.reshape(v.shape[:-1] + (-1, 32))
    amax = np.abs(blocks).max(-1, keepdims=True)
    byte = np.maximum(np.where(amax > 0, np.frexp(amax)[1] - 1 + 127, 0) - down, 1)
    scale = np.exp2(byte - 127.0)
    codes = (blocks / scale).astype(np.float32).astype(dtype).astype(np.float64)
    return np.moveaxis((codes * scale).reshape(v.shape), -1, axis)


WIDE = False


def mx_kscale(k):
    if not WIDE:
        return np.ones(k)
    levels = np.array([10, -10, 5, -5, 0])
    if k % 512:
        return np.exp2(np.random.permutation(np.resize(levels, k // 32))).repeat(32)
    a = np.empty((k // 512, 16))
    for p in range(k // 512):
        a[p, :8] = np.random.permutation(np.resize(levels, 8))
        for g in range(8):
            far = levels[np.abs(levels - a[p, g]) >= 10]
            a[p, g + 8] = far[np.random.randint(len(far))]
    return np.exp2(a.ravel()).repeat(32)


def f64(x):
    return np.asarray(x).astype(np.float64)


def striped8(idx):
    return np.asarray(idx).reshape(8, -1, 16).transpose(0, 2, 1).reshape(128, -1).astype(np.uint16)


def unstriped8(offs):
    return offs.reshape(8, 16, -1).transpose(0, 2, 1).reshape(8, -1).astype(np.int64)


def pick8(x, idx, run):
    r = np.arange(len(x))
    return x[r[:, None], idx[r % (8 * run) // run]]


E2M1 = np.array([0.0, 0.5, 1.0, 1.5, 2.0, 3.0, 4.0, 6.0, -0.0, -0.5, -1.0, -1.5, -2.0, -3.0, -4.0, -6.0])


def pack_weight(w, fmt):
    k, n = w.shape
    w = f64(np.asarray(w, np.float32).astype(ml_dtypes.bfloat16)).reshape(k // 32, 32, n)
    amax = np.abs(w).max(1)
    if fmt == "e4m3":
        byte = np.frexp(amax)[1] - 1 + 127 - 7
    else:
        mant, ex = np.frexp(amax / 6.0)
        byte = np.where(mant > 0.5, ex, ex - 1) + 127
    byte = np.clip(np.where(amax > 0, byte, 1), 1, 254)
    scaled = (w * np.exp2(127.0 - byte)[:, None, :]).reshape(k, n).astype(np.float32)
    by_word = np.ascontiguousarray(scaled.reshape(k // 512, 128, 4, n).transpose(0, 1, 3, 2))
    if fmt == "e4m3":
        words = by_word.astype(ml_dtypes.float8_e4m3fn).view(np.uint8)
    else:
        c = by_word.astype(ml_dtypes.float4_e2m1fn).view(np.uint8) & 0xF
        words = (c[..., 0::2] | (c[..., 1::2] << 4)).reshape(k // 512, 128, 2 * n)
    return np.ascontiguousarray(words), np.ascontiguousarray(byte.astype(np.uint8).reshape(k // 512, 16, n))


def unpack_weight(words, scales, fmt):
    g, _, n = scales.shape
    words = np.ascontiguousarray(words).reshape(g, 128, n, -1)
    if fmt == "e4m3":
        vals = words.view(ml_dtypes.float8_e4m3fn).astype(np.float64)
    else:
        nib = np.empty((g, 128, n, 4), np.uint8)
        nib[..., 0::2] = words & 0xF
        nib[..., 1::2] = words >> 4
        vals = E2M1[nib]
    vals = vals * np.repeat(np.exp2(scales.astype(np.float64) - 127.0), 8, axis=1)[..., None]
    return vals.transpose(0, 1, 3, 2).reshape(g * 512, n)


K, T, J, N = 1024, 2048, 512, 512


def setup_inputs():
    n = np.random.standard_normal
    idx = np.stack([np.random.permutation(T)[:J] for _ in range(8)])
    fk = mx_kscale(K)
    xqp = pack_weight(n((K, T)) / fk[:, None], "e2m1")
    wap = pack_weight(n((K, N)) * 1 / np.sqrt(K) * fk[:, None], "e2m1")
    wrp = pack_weight(n((K, N)) * 1 / np.sqrt(K) * fk[:, None], "e4m3")
    return {
        "xq_words": xqp[0],
        "xq_scales": xqp[1],
        "wa_words": wap[0],
        "wa_scales": wap[1],
        "rq": (n((K, J)) * 0.5 / fk[:, None]).astype(np.float32),
        "wr_words": wrp[0],
        "wr_scales": wrp[1],
        "gm": (np.random.uniform(0.5, 2.0, (N, 1))).astype(np.float32),
        "offs": striped8(idx),
    }


def reference(xq_words, xq_scales, wa_words, wa_scales, rq, wr_words, wr_scales, gm, offs):
    idx = unstriped8(offs)
    xqu = unpack_weight(xq_words, xq_scales, "e2m1")
    wau = unpack_weight(wa_words, wa_scales, "e2m1")
    wru = unpack_weight(wr_words, wr_scales, "e4m3")
    z = wau.T @ xqu
    rqq = mxq(f64(rq), 0, "e4m3")
    p = wru.T @ rqq
    pf = p * f64(gm)
    pg = np.zeros((N, T))
    pg[np.arange(N)[:, None], idx[np.arange(N) % 512 // 64]] = pf
    y = np.maximum(z + pg, 0.0)
    return y

@@ -1,0 +1,232 @@
+from contextlib import ExitStack
+
+import concourse.mybir as mybir
+from concourse.masks import make_identity
+
+K, T, J, N = 1024, 2048, 512, 512
+FLOPS = 2 * K * N * (T + J)
+
+F32 = mybir.dt.float32
+BF16 = mybir.dt.bfloat16
+I32 = mybir.dt.int32
+U32 = mybir.dt.uint32
+U16 = mybir.dt.uint16
+U8 = mybir.dt.uint8
+FP8X4 = mybir.dt.float8_e4m3fn_x4
+FP4X4 = mybir.dt.float4_e2m1fn_x4
+ACT = mybir.ActivationFunctionType
+ALU = mybir.AluOpType
+
+P = 128
+PASSES = 2
+TILES = 4
+BANK = 512
+CHUNKS = T // BANK
+HALF = J // 2
+GPSIMD_CHUNKS = (2, 3, 3, 1)
+
+
+def tile_list_head_patches_kernel(tc, xq_words, xq_scales, wa_words, wa_scales, rq, wr_words, wr_scales, gm, offs, out):
+    nc = tc.nc
+    with ExitStack() as ctx:
+        lists = ctx.enter_context(tc.tile_pool(name="lists", bufs=1))
+        keep = ctx.enter_context(tc.tile_pool(name="keep", bufs=1))
+        stage = ctx.enter_context(tc.tile_pool(name="stage", bufs=1))
+        psum_p = ctx.enter_context(tc.psum_pool(name="psum_p", bufs=2))
+        psum_g = ctx.enter_context(tc.psum_pool(name="psum_g", bufs=2))
+        psum_v = ctx.enter_context(tc.psum_pool(name="psum_v", bufs=4))
+
+        def sbuf(name, shape, dtype, after=None):
+            return keep.tile(shape, dtype, name=name, tag=after or name, align_bytes=64)
+
+        def staged(name, shape, dtype, offset):
+            return stage.tile(shape, dtype, name=name, offset=offset, align_bytes=64)
+
+        offsets = lists.tile([P, J // 16], U16, name="offsets")
+        nc.sync.dma_start(offsets[:], offs)
+
+        gain_rows = sbuf("gain_rows", [P, P], F32)
+        wr_scales_raw = sbuf("wr_scales_raw", [P, PASSES, N], U8)
+        identity = sbuf("identity", [P, P], F32)
+        nc.gpsimd.memset(gain_rows[:], 0.0)
+        nc.gpsimd.memset(wr_scales_raw[:].bitcast(I32), 0)
+        pages = [sbuf(f"page{g}", [P, T], F32) for g in range(2)]
+        nc.vector.memset(pages[0][:, 0 : T - 1], 0.0)
+        nc.vector.memset(pages[0][:, T - 1 : T], 0.0)
+        nc.gpsimd.memset(pages[1][:], 0.0)
+        make_identity(nc, identity[:])
+
+        def load_scale_rows(queue, plane, scales):
+            for q in range(4):
+                queue.dma_start(
+                    out=plane[32 * q : 32 * q + 4, :, :].bitcast(I32),
+                    in_=scales[:, 4 * q : 4 * q + 4, :].rearrange("z r c -> r z c").bitcast(I32),
+                )
+
+        rq_rows = rq.rearrange("(z p r) j -> z p r j", z=PASSES, r=4)
+        rq_raw = {}
+
+        def load_rq(h, z):
+            raw = staged(f"rq_raw{h}{z}", [P, 4, HALF], F32, 4096 * z)
+            nc.sync.dma_start(out=raw[:], in_=rq_rows[z][:, :, h * HALF : (h + 1) * HALF])
+            rq_raw[h, z] = raw
+
+        load_rq(0, 0)
+        load_rq(0, 1)
+        wr_raw = staged("wr_raw", [P, PASSES, N], I32, 12288)
+        nc.sync.dma_start(out=wr_raw[:], in_=wr_words.rearrange("z p n t -> p z (n t)").bitcast(I32))
+        nc.scalar.dma_start(
+            out=gain_rows[0:TILES, :].rearrange("i (u b) -> i u b", b=4),
+            in_=gm.rearrange("(u i b) o -> i u (b o)", i=TILES, b=4),
+        )
+        load_scale_rows(nc.scalar, wr_scales_raw, wr_scales)
+        gains_t = psum_p.tile([P, P], F32, name="acc_p")
+        nc.tensor.transpose(gains_t[:], gain_rows[:], identity[:])
+        gains = sbuf("gains", [P, TILES], F32)
+        nc.scalar.activation(out=gains[:], in_=gains_t[:, 0:TILES], func=ACT.Copy)
+
+        rq_codes = [sbuf(f"rq_codes{z}", [P, J], U32) for z in range(PASSES)]
+        rq_plane = [sbuf(f"rq_plane{z}", [P, J], U8) for z in range(PASSES)]
+        rq_bf = {}
+
+        def round_rq(h, z):
+            name, shape = f"rq_bf{h}{z}", [P, HALF, 4]
+            woven = staged(name, shape, BF16, 8192) if (h, z) == (0, 1) else sbuf(name, shape, BF16)
+            dst = woven[:].rearrange("p (c i) t -> p c t i", i=4)
+            src = rq_raw[h, z][:].rearrange("p t (c i) -> p c t i", i=4)
+            if h == 0:
+                nc.vector.tensor_copy(out=dst, in_=src)
+            else:
+                nc.scalar.activation(out=dst, in_=src, func=ACT.Copy)
+            rq_bf[h, z] = woven
+
+        def quantise_rq(h, z):
+            cols = slice(h * HALF, (h + 1) * HALF)
+            nc.vector.quantize_mx(
+                out=rq_codes[z][:, cols].bitcast(FP8X4),
+                scales=rq_plane[z][:, cols],
+                in_=rq_bf[h, z][:].rearrange("p c t -> p (c t)"),
+            )
+
+        for z in range(PASSES):
+            round_rq(0, z)
+            load_rq(1, z)
+            quantise_rq(0, z)
+
+        wa_raw = staged("wa_raw", [P, PASSES, N // 2], I32, 8192)
+        nc.sync.dma_start(out=wa_raw[:], in_=wa_words.rearrange("z p b -> p z b").bitcast(I32))
+
+        wr_plane = sbuf("wr_plane", [P, PASSES, TILES, P], U8)
+        wr_codes = [sbuf(f"wr_codes{g}", [P, PASSES, 2, P], I32) for g in range(2)]
+        wr_dealt = wr_raw[:].rearrange("p z (u i b) -> p z i u b", i=TILES, b=4)
+
+        def deal_wr(g):
+            nc.vector.tensor_copy(
+                out=wr_codes[g][:].rearrange("p z i (u b) -> p z i u b", b=4),
+                in_=wr_dealt[:, :, 2 * g : 2 * g + 2],
+            )
+
+        def deal_scales(plane, raw):
+            nc.vector.tensor_copy(
+                out=plane[:].bitcast(I32),
+                in_=raw[:].bitcast(I32).rearrange("p z (u i) -> p z i u", i=TILES),
+            )
+
+        deal_scales(wr_plane, wr_scales_raw)
+        load_scale_rows(nc.sync, wr_scales_raw, wa_scales)
+        deal_wr(0)
+        deal_wr(1)
+
+        xq_view = xq_words.rearrange("z p b -> p z b")
+        xq_codes = staged("xq_codes", [P, PASSES, 2 * T], U8, 14336)
+        nc.sync.dma_start(out=xq_codes[:].bitcast(I32), in_=xq_view.bitcast(I32))
+        xq_plane = staged("xq_plane", [P, PASSES, T], U8, 10240)
+        nc.vector.memset(xq_plane[:].bitcast(I32), 0)
+        load_scale_rows(nc.sync, xq_plane, xq_scales)
+
+        def patch_product(i, cols):
+            acc = psum_p.tile([P, cols.stop - cols.start], F32, name="acc_p")
+            for z in range(PASSES):
+                nc.tensor.matmul_mx(
+                    out=acc[:],
+                    lhsT=wr_codes[i // 2][:, z, i % 2, :].bitcast(FP8X4),
+                    lhsT_scale=wr_plane[:, z, i, :],
+                    rhs=rq_codes[z][:, cols].bitcast(FP8X4),
+                    rhs_scale=rq_plane[z][:, cols],
+                    start=(z == 0),
+                    stop=(z == PASSES - 1),
+                )
+            return acc
+
+        def scale_patches(i, cols, acc, offset):
+            name, shape = f"patches{i}_{cols.start}", [P, cols.stop - cols.start]
+            patches = sbuf(name, shape, F32) if offset is None else staged(name, shape, F32, offset)
+            nc.scalar.activation(out=patches[:], in_=acc[:], func=ACT.Copy, scale=gains[:, i : i + 1])
+            return patches
+
+        def place(i, cols, patches):
+            entries = offsets[:, cols.start // 16 : cols.stop // 16]
+            nc.vector.tensor_copy(pages[i % 2][:].indirect(entries), patches[:])
+
+        first, second, whole = slice(0, HALF), slice(HALF, J), slice(0, J)
+        patches_first0 = sbuf("patches_first0", [P, HALF], F32)
+        nc.vector.tensor_scalar(
+            out=patches_first0[:], in0=patch_product(0, first)[:], scalar1=gains[:, 0:1], scalar2=None, op0=ALU.mult
+        )
+        place(0, first, patches_first0)
+        acc_first1 = patch_product(1, first)
+        round_rq(1, 0)
+        round_rq(1, 1)
+        for z in range(PASSES):
+            quantise_rq(1, z)
+
+        wa_plane = sbuf("wa_plane", [P, PASSES, TILES, P], U8)
+        wa_codes = sbuf("wa_codes", [P, PASSES, TILES, 2 * P], U8, "wr_scales_raw")
+        deal_scales(wa_plane, wr_scales_raw)
+        nc.vector.tensor_copy(
+            out=wa_codes[:].bitcast(I32).rearrange("p z i (u w) -> p z i u w", w=2),
+            in_=wa_raw[:].rearrange("p z (u i w) -> p z i u w", i=TILES, w=2),
+        )
+        place(1, first, scale_patches(1, first, acc_first1, 7680))
+        place(0, second, scale_patches(0, second, patch_product(0, second), 9216))
+        place(1, second, scale_patches(1, second, patch_product(1, second), None))
+        later_patches = {i: scale_patches(i, whole, patch_product(i, whole), None) for i in (2, 3)}
+
+        out_rows = out.rearrange("(u i b) t -> i u b t", i=TILES, b=4)
+
+        def token_product(i, c):
+            acc = (psum_g if c < GPSIMD_CHUNKS[i] else psum_v).tile([P, BANK], F32, name="acc_z")
+            for z in range(PASSES):
+                b0 = c * 2 * BANK
+                nc.tensor.matmul_mx(
+                    out=acc[:],
+                    lhsT=wa_codes[:, z, i, :].bitcast(FP4X4),
+                    lhsT_scale=wa_plane[:, z, i, :],
+                    rhs=xq_codes[:, z, b0 : b0 + 2 * BANK].bitcast(FP4X4),
+                    rhs_scale=xq_plane[:, z, c * BANK : (c + 1) * BANK],
+                    start=(z == 0),
+                    stop=(z == PASSES - 1),
+                )
+            if c < GPSIMD_CHUNKS[i]:
+                held = sbuf(f"held{i}{c}", [P, BANK], F32)
+                nc.scalar.copy(out=held[:], in_=acc[:])
+                return held
+            return acc
+
+        def finish(i, c, sums):
+            cols = slice(c * BANK, (c + 1) * BANK)
+            total = sbuf(f"total{i}{c}", [P, BANK], F32)
+            engine = nc.gpsimd if c < GPSIMD_CHUNKS[i] else nc.vector
+            engine.tensor_tensor(out=total[:], in0=sums[:], in1=pages[i % 2][:, cols], op=ALU.add)
+            result = sbuf(f"result{i}{c}", [P, BANK], F32, {(1, 3): "total12", (2, 3): "total22", (3, 1): "total23"}.get((i, c)))
+            nc.scalar.activation(out=result[:], in_=total[:], func=ACT.Relu)
+            nc.sync.dma_start(out=out_rows[i][:, :, cols], in_=result[:])
+
+        sums = {0: [token_product(0, c) for c in range(CHUNKS)]}
+        for i in range(TILES):
+            if i + 1 < TILES:
+                sums[i + 1] = [token_product(i + 1, c) for c in range(CHUNKS)]
+            if i >= 2:
+                place(i, whole, later_patches[i])
+            for c in range(CHUNKS):
+                finish(i, c, sums[i][c])

@@ -47,14 +47,20 @@ def tile_list_head_patches_kernel(tc, xq_words, xq_scales, wa_words, wa_scales, 
 
         gain_rows = sbuf("gain_rows", [P, P], F32)
         wr_scales_raw = sbuf("wr_scales_raw", [P, PASSES, N], U8)
+        wa_scales_raw = sbuf("wa_scales_raw", [P, PASSES, N], U8)
+        xq_plane = sbuf("xq_plane", [P, PASSES, T], U8)
         identity = sbuf("identity", [P, P], F32)
         nc.gpsimd.memset(gain_rows[:], 0.0)
         nc.gpsimd.memset(wr_scales_raw[:].bitcast(I32), 0)
+        nc.gpsimd.memset(wa_scales_raw[:].bitcast(I32), 0)
+        make_identity(nc, identity[:])
         pages = [sbuf(f"page{g}", [P, T], F32) for g in range(2)]
         nc.vector.memset(pages[0][:, 0 : T - 1], 0.0)
         nc.vector.memset(pages[0][:, T - 1 : T], 0.0)
         nc.gpsimd.memset(pages[1][:], 0.0)
-        make_identity(nc, identity[:])
+        plane_words = xq_plane[:].rearrange("p z c -> p (z c)").bitcast(I32)
+        nc.vector.memset(plane_words[:, 0 : T // 2 - 1], 0)
+        nc.vector.memset(plane_words[:, T // 2 - 1 : T // 2], 0)
 
         def load_scale_rows(queue, plane, scales):
             for q in range(4):
@@ -67,31 +73,38 @@ def tile_list_head_patches_kernel(tc, xq_words, xq_scales, wa_words, wa_scales, 
         rq_raw = {}
 
         def load_rq(h, z):
-            raw = staged(f"rq_raw{h}{z}", [P, 4, HALF], F32, 4096 * z)
+            raw = sbuf(f"rq_raw{h}{z}", [P, 4, HALF], F32)
             nc.sync.dma_start(out=raw[:], in_=rq_rows[z][:, :, h * HALF : (h + 1) * HALF])
             rq_raw[h, z] = raw
 
-        load_rq(0, 0)
-        load_rq(0, 1)
-        wr_raw = staged("wr_raw", [P, PASSES, N], I32, 12288)
-        nc.sync.dma_start(out=wr_raw[:], in_=wr_words.rearrange("z p n t -> p z (n t)").bitcast(I32))
-        nc.scalar.dma_start(
+        nc.sync.dma_start(
             out=gain_rows[0:TILES, :].rearrange("i (u b) -> i u b", b=4),
             in_=gm.rearrange("(u i b) o -> i u (b o)", i=TILES, b=4),
         )
-        load_scale_rows(nc.scalar, wr_scales_raw, wr_scales)
+        load_rq(0, 0)
+        load_rq(0, 1)
+        load_scale_rows(nc.sync, wr_scales_raw, wr_scales)
+        wr_raw = sbuf("wr_raw", [P, PASSES, N], I32)
+        nc.sync.dma_start(out=wr_raw[:], in_=wr_words.rearrange("z p n t -> p z (n t)").bitcast(I32))
+        load_rq(1, 0)
+        load_rq(1, 1)
+        wa_raw = staged("wa_raw", [P, PASSES, N // 2], I32, 1024)
+        nc.sync.dma_start(out=wa_raw[:], in_=wa_words.rearrange("z p b -> p z b").bitcast(I32))
+        load_scale_rows(nc.sync, wa_scales_raw, wa_scales)
+        xq_codes = sbuf("xq_codes", [P, PASSES, 2 * T], U8)
+        nc.sync.dma_start(out=xq_codes[:].bitcast(I32), in_=xq_words.rearrange("z p b -> p z b").bitcast(I32))
+        load_scale_rows(nc.sync, xq_plane, xq_scales)
         gains_t = psum_p.tile([P, P], F32, name="acc_p")
         nc.tensor.transpose(gains_t[:], gain_rows[:], identity[:])
         gains = sbuf("gains", [P, TILES], F32)
-        nc.scalar.activation(out=gains[:], in_=gains_t[:, 0:TILES], func=ACT.Copy)
+        nc.vector.tensor_copy(out=gains[:], in_=gains_t[:, 0:TILES])
 
-        rq_codes = [sbuf(f"rq_codes{z}", [P, J], U32) for z in range(PASSES)]
+        rq_codes = {}
         rq_plane = [sbuf(f"rq_plane{z}", [P, J], U8) for z in range(PASSES)]
         rq_bf = {}
 
         def round_rq(h, z):
-            name, shape = f"rq_bf{h}{z}", [P, HALF, 4]
-            woven = staged(name, shape, BF16, 8192) if (h, z) == (0, 1) else sbuf(name, shape, BF16)
+            woven = sbuf(f"rq_bf{h}{z}", [P, HALF, 4], BF16)
             dst = woven[:].rearrange("p (c i) t -> p c t i", i=4)
             src = rq_raw[h, z][:].rearrange("p t (c i) -> p c t i", i=4)
             if h == 0:
@@ -102,19 +115,18 @@ def tile_list_head_patches_kernel(tc, xq_words, xq_scales, wa_words, wa_scales, 
 
         def quantise_rq(h, z):
             cols = slice(h * HALF, (h + 1) * HALF)
+            name, shape = f"rq_codes{h}{z}", [P, HALF]
+            rq_codes[h, z] = staged(name, shape, U32, 1536 + 1024 * z) if h else sbuf(name, shape, U32)
             nc.vector.quantize_mx(
-                out=rq_codes[z][:, cols].bitcast(FP8X4),
+                out=rq_codes[h, z][:].bitcast(FP8X4),
                 scales=rq_plane[z][:, cols],
                 in_=rq_bf[h, z][:].rearrange("p c t -> p (c t)"),
             )
 
         for z in range(PASSES):
             round_rq(0, z)
-            load_rq(1, z)
             quantise_rq(0, z)
 
-        wa_raw = staged("wa_raw", [P, PASSES, N // 2], I32, 8192)
-        nc.sync.dma_start(out=wa_raw[:], in_=wa_words.rearrange("z p b -> p z b").bitcast(I32))
 
         wr_plane = sbuf("wr_plane", [P, PASSES, TILES, P], U8)
         wr_codes = [sbuf(f"wr_codes{g}", [P, PASSES, 2, P], I32) for g in range(2)]
@@ -133,29 +145,22 @@ def tile_list_head_patches_kernel(tc, xq_words, xq_scales, wa_words, wa_scales, 
             )
 
         deal_scales(wr_plane, wr_scales_raw)
-        load_scale_rows(nc.sync, wr_scales_raw, wa_scales)
         deal_wr(0)
         deal_wr(1)
 
-        xq_view = xq_words.rearrange("z p b -> p z b")
-        xq_codes = staged("xq_codes", [P, PASSES, 2 * T], U8, 14336)
-        nc.sync.dma_start(out=xq_codes[:].bitcast(I32), in_=xq_view.bitcast(I32))
-        xq_plane = staged("xq_plane", [P, PASSES, T], U8, 10240)
-        nc.vector.memset(xq_plane[:].bitcast(I32), 0)
-        load_scale_rows(nc.sync, xq_plane, xq_scales)
-
         def patch_product(i, cols):
             acc = psum_p.tile([P, cols.stop - cols.start], F32, name="acc_p")
-            for z in range(PASSES):
-                nc.tensor.matmul_mx(
-                    out=acc[:],
-                    lhsT=wr_codes[i // 2][:, z, i % 2, :].bitcast(FP8X4),
-                    lhsT_scale=wr_plane[:, z, i, :],
-                    rhs=rq_codes[z][:, cols].bitcast(FP8X4),
-                    rhs_scale=rq_plane[z][:, cols],
-                    start=(z == 0),
-                    stop=(z == PASSES - 1),
-                )
+            for j0 in range(cols.start, cols.stop, HALF):
+                for z in range(PASSES):
+                    nc.tensor.matmul_mx(
+                        out=acc[:, j0 - cols.start : j0 - cols.start + HALF],
+                        lhsT=wr_codes[i // 2][:, z, i % 2, :].bitcast(FP8X4),
+                        lhsT_scale=wr_plane[:, z, i, :],
+                        rhs=rq_codes[j0 // HALF, z][:].bitcast(FP8X4),
+                        rhs_scale=rq_plane[z][:, j0 : j0 + HALF],
+                        start=(z == 0),
+                        stop=(z == PASSES - 1),
+                    )
             return acc
 
         def scale_patches(i, cols, acc, offset):
@@ -177,18 +182,18 @@ def tile_list_head_patches_kernel(tc, xq_words, xq_scales, wa_words, wa_scales, 
         acc_first1 = patch_product(1, first)
         round_rq(1, 0)
         round_rq(1, 1)
-        for z in range(PASSES):
-            quantise_rq(1, z)
 
         wa_plane = sbuf("wa_plane", [P, PASSES, TILES, P], U8)
-        wa_codes = sbuf("wa_codes", [P, PASSES, TILES, 2 * P], U8, "wr_scales_raw")
-        deal_scales(wa_plane, wr_scales_raw)
+        wa_codes = sbuf("wa_codes", [P, PASSES, TILES, 2 * P], U8, "wa_scales_raw")
+        deal_scales(wa_plane, wa_scales_raw)
         nc.vector.tensor_copy(
             out=wa_codes[:].bitcast(I32).rearrange("p z i (u w) -> p z i u w", w=2),
             in_=wa_raw[:].rearrange("p z (u i w) -> p z i u w", i=TILES, w=2),
         )
-        place(1, first, scale_patches(1, first, acc_first1, 7680))
-        place(0, second, scale_patches(0, second, patch_product(0, second), 9216))
+        for z in range(PASSES):
+            quantise_rq(1, z)
+        place(1, first, scale_patches(1, first, acc_first1, 512))
+        place(0, second, scale_patches(0, second, patch_product(0, second), None))
         place(1, second, scale_patches(1, second, patch_product(1, second), None))
         later_patches = {i: scale_patches(i, whole, patch_product(i, whole), None) for i in (2, 3)}
 
@@ -219,7 +224,14 @@ def tile_list_head_patches_kernel(tc, xq_words, xq_scales, wa_words, wa_scales, 
             engine = nc.gpsimd if c < GPSIMD_CHUNKS[i] else nc.vector
             engine.tensor_tensor(out=total[:], in0=sums[:], in1=pages[i % 2][:, cols], op=ALU.add)
             result = sbuf(f"result{i}{c}", [P, BANK], F32, {(1, 3): "total12", (2, 3): "total22", (3, 1): "total23"}.get((i, c)))
-            nc.scalar.activation(out=result[:], in_=total[:], func=ACT.Relu)
+            if (i, c) == (3, 0):
+                engine.tensor_scalar(
+                    out=result[:], in0=total[:], scalar1=3.4028234663852886e38, scalar2=0.0, op0=ALU.min, op1=ALU.max
+                )
+            elif (i, c) == (3, 3):
+                engine.tensor_scalar(out=result[:], in0=total[:], scalar1=0.0, scalar2=None, op0=ALU.max)
+            else:
+                nc.scalar.activation(out=result[:], in_=total[:], func=ACT.Relu)
             nc.sync.dma_start(out=out_rows[i][:, :, cols], in_=result[:])
 
         sums = {0: [token_product(0, c) for c in range(CHUNKS)]}

@@ -32,8 +32,7 @@ def tile_list_head_patches_kernel(tc, xq_words, xq_scales, wa_words, wa_scales, 
         lists = ctx.enter_context(tc.tile_pool(name="lists", bufs=1))
         keep = ctx.enter_context(tc.tile_pool(name="keep", bufs=1))
         stage = ctx.enter_context(tc.tile_pool(name="stage", bufs=1))
-        psum_p = ctx.enter_context(tc.psum_pool(name="psum_p", bufs=2))
-        psum_g = ctx.enter_context(tc.psum_pool(name="psum_g", bufs=2))
+        psum_p = ctx.enter_context(tc.psum_pool(name="psum_p", bufs=4))
         psum_v = ctx.enter_context(tc.psum_pool(name="psum_v", bufs=4))
 
         def sbuf(name, shape, dtype, after=None):
@@ -96,8 +95,10 @@ def tile_list_head_patches_kernel(tc, xq_words, xq_scales, wa_words, wa_scales, 
         load_scale_rows(nc.sync, xq_plane, xq_scales)
         gains_t = psum_p.tile([P, P], F32, name="acc_p")
         nc.tensor.transpose(gains_t[:], gain_rows[:], identity[:])
-        gains = sbuf("gains", [P, TILES], F32)
-        nc.vector.tensor_copy(out=gains[:], in_=gains_t[:, 0:TILES])
+        gains = sbuf("gains", [P, TILES - 1], F32)
+        nc.vector.tensor_copy(out=gains[:], in_=gains_t[:, 0 : TILES - 1])
+        last_gain = sbuf("last_gain", [P, 1], F32)
+        nc.vector.tensor_copy(out=last_gain[:], in_=gains_t[:, TILES - 1 : TILES])
 
         rq_codes = {}
         rq_plane = [sbuf(f"rq_plane{z}", [P, J], U8) for z in range(PASSES)]
@@ -166,7 +167,7 @@ def tile_list_head_patches_kernel(tc, xq_words, xq_scales, wa_words, wa_scales, 
         def scale_patches(i, cols, acc, offset):
             name, shape = f"patches{i}_{cols.start}", [P, cols.stop - cols.start]
             patches = sbuf(name, shape, F32) if offset is None else staged(name, shape, F32, offset)
-            nc.scalar.activation(out=patches[:], in_=acc[:], func=ACT.Copy, scale=gains[:, i : i + 1])
+            nc.scalar.activation(out=patches[:], in_=acc[:], func=ACT.Copy, scale=gains[:, i : i + 1] if i + 1 < TILES else last_gain[:])
             return patches
 
         def place(i, cols, patches):
@@ -195,12 +196,11 @@ def tile_list_head_patches_kernel(tc, xq_words, xq_scales, wa_words, wa_scales, 
         place(1, first, scale_patches(1, first, acc_first1, 512))
         place(0, second, scale_patches(0, second, patch_product(0, second), None))
         place(1, second, scale_patches(1, second, patch_product(1, second), None))
-        later_patches = {i: scale_patches(i, whole, patch_product(i, whole), None) for i in (2, 3)}
 
         out_rows = out.rearrange("(u i b) t -> i u b t", i=TILES, b=4)
 
         def token_product(i, c):
-            acc = (psum_g if c < GPSIMD_CHUNKS[i] else psum_v).tile([P, BANK], F32, name="acc_z")
+            acc = (psum_p if c < GPSIMD_CHUNKS[i] else psum_v).tile([P, BANK], F32, name="acc_p")
             for z in range(PASSES):
                 b0 = c * 2 * BANK
                 nc.tensor.matmul_mx(
@@ -218,12 +218,24 @@ def tile_list_head_patches_kernel(tc, xq_words, xq_scales, wa_words, wa_scales, 
                 return held
             return acc
 
+        relu_order = []
+
         def finish(i, c, sums):
             cols = slice(c * BANK, (c + 1) * BANK)
-            total = sbuf(f"total{i}{c}", [P, BANK], F32)
+            name, shape = f"total{i}{c}", [P, BANK]
+            total = staged(name, shape, F32, 5120) if (i, c) == (0, 0) else sbuf(name, shape, F32)
             engine = nc.gpsimd if c < GPSIMD_CHUNKS[i] else nc.vector
             engine.tensor_tensor(out=total[:], in0=sums[:], in1=pages[i % 2][:, cols], op=ALU.add)
-            result = sbuf(f"result{i}{c}", [P, BANK], F32, {(1, 3): "total12", (2, 3): "total22", (3, 1): "total23"}.get((i, c)))
+            on_scalar = (i, c) not in ((3, 0), (3, 3))
+            name = f"result{i}{c}"
+            if (i, c) in ((0, 1), (0, 2)):
+                result = staged(name, shape, F32, 2048 + 2048 * c)
+            elif (i, c) == (0, 0):
+                result = sbuf(name, shape, F32, "gains")
+            else:
+                result = sbuf(name, shape, F32, relu_order[-2] if on_scalar else None)
+            if on_scalar:
+                relu_order.append(f"total{i}{c}")
             if (i, c) == (3, 0):
                 engine.tensor_scalar(
                     out=result[:], in0=total[:], scalar1=3.4028234663852886e38, scalar2=0.0, op0=ALU.min, op1=ALU.max
@@ -234,11 +246,18 @@ def tile_list_head_patches_kernel(tc, xq_words, xq_scales, wa_words, wa_scales, 
                 nc.scalar.activation(out=result[:], in_=total[:], func=ACT.Relu)
             nc.sync.dma_start(out=out_rows[i][:, :, cols], in_=result[:])
 
-        sums = {0: [token_product(0, c) for c in range(CHUNKS)]}
+        sums = {}
+        later_patches = {}
         for i in range(TILES):
-            if i + 1 < TILES:
-                sums[i + 1] = [token_product(i + 1, c) for c in range(CHUNKS)]
+            for c in range(GPSIMD_CHUNKS[i]):
+                sums[i, c] = token_product(i, c)
+            if i >= 1:
+                for c in range(GPSIMD_CHUNKS[i - 1], CHUNKS):
+                    sums[i - 1, c] = token_product(i - 1, c)
+            if i + 2 < TILES:
+                later_patches[i + 2] = scale_patches(i + 2, whole, patch_product(i + 2, whole), None)
+        for i in range(TILES):
             if i >= 2:
                 place(i, whole, later_patches[i])
             for c in range(CHUNKS):
-                finish(i, c, sums[i][c])
+                finish(i, c, sums[i, c] if (i, c) in sums else token_product(i, c))

from contextlib import ExitStack

import concourse.mybir as mybir
from concourse.masks import make_identity

K, T, J, N = 1024, 2048, 512, 512
FLOPS = 2 * K * N * (T + J)

F32 = mybir.dt.float32
BF16 = mybir.dt.bfloat16
I32 = mybir.dt.int32
U32 = mybir.dt.uint32
U16 = mybir.dt.uint16
U8 = mybir.dt.uint8
FP8X4 = mybir.dt.float8_e4m3fn_x4
FP4X4 = mybir.dt.float4_e2m1fn_x4
ACT = mybir.ActivationFunctionType
ALU = mybir.AluOpType

P = 128
PASSES = 2
TILES = 4
BANK = 512
CHUNKS = T // BANK
HALF = J // 2
GPSIMD_CHUNKS = (2, 3, 3, 1)


def tile_list_head_patches_kernel(tc, xq_words, xq_scales, wa_words, wa_scales, rq, wr_words, wr_scales, gm, offs, out):
    nc = tc.nc
    with ExitStack() as ctx:
        lists = ctx.enter_context(tc.tile_pool(name="lists", bufs=1))
        keep = ctx.enter_context(tc.tile_pool(name="keep", bufs=1))
        stage = ctx.enter_context(tc.tile_pool(name="stage", bufs=1))
        psum_p = ctx.enter_context(tc.psum_pool(name="psum_p", bufs=4))
        psum_v = ctx.enter_context(tc.psum_pool(name="psum_v", bufs=4))

        def sbuf(name, shape, dtype, after=None):
            return keep.tile(shape, dtype, name=name, tag=after or name, align_bytes=64)

        def staged(name, shape, dtype, offset):
            return stage.tile(shape, dtype, name=name, offset=offset, align_bytes=64)

        offsets = lists.tile([P, J // 16], U16, name="offsets")
        nc.sync.dma_start(offsets[:], offs)

        gain_rows = sbuf("gain_rows", [P, P], F32)
        wr_scales_raw = sbuf("wr_scales_raw", [P, PASSES, N], U8)
        wa_scales_raw = sbuf("wa_scales_raw", [P, PASSES, N], U8)
        xq_plane = sbuf("xq_plane", [P, PASSES, T], U8)
        identity = sbuf("identity", [P, P], F32)
        nc.gpsimd.memset(gain_rows[:], 0.0)
        nc.gpsimd.memset(wr_scales_raw[:].bitcast(I32), 0)
        nc.gpsimd.memset(wa_scales_raw[:].bitcast(I32), 0)
        make_identity(nc, identity[:])
        pages = [sbuf(f"page{g}", [P, T], F32) for g in range(2)]
        nc.vector.memset(pages[0][:, 0 : T - 1], 0.0)
        nc.vector.memset(pages[0][:, T - 1 : T], 0.0)
        nc.gpsimd.memset(pages[1][:], 0.0)
        plane_words = xq_plane[:].rearrange("p z c -> p (z c)").bitcast(I32)
        nc.vector.memset(plane_words[:, 0 : T // 2 - 1], 0)
        nc.vector.memset(plane_words[:, T // 2 - 1 : T // 2], 0)

        def load_scale_rows(queue, plane, scales):
            for q in range(4):
                queue.dma_start(
                    out=plane[32 * q : 32 * q + 4, :, :].bitcast(I32),
                    in_=scales[:, 4 * q : 4 * q + 4, :].rearrange("z r c -> r z c").bitcast(I32),
                )

        rq_rows = rq.rearrange("(z p r) j -> z p r j", z=PASSES, r=4)
        rq_raw = {}

        def load_rq(h, z):
            raw = sbuf(f"rq_raw{h}{z}", [P, 4, HALF], F32)
            nc.sync.dma_start(out=raw[:], in_=rq_rows[z][:, :, h * HALF : (h + 1) * HALF])
            rq_raw[h, z] = raw

        nc.sync.dma_start(
            out=gain_rows[0:TILES, :].rearrange("i (u b) -> i u b", b=4),
            in_=gm.rearrange("(u i b) o -> i u (b o)", i=TILES, b=4),
        )
        load_rq(0, 0)
        load_rq(0, 1)
        load_scale_rows(nc.sync, wr_scales_raw, wr_scales)
        wr_raw = sbuf("wr_raw", [P, PASSES, N], I32)
        nc.sync.dma_start(out=wr_raw[:], in_=wr_words.rearrange("z p n t -> p z (n t)").bitcast(I32))
        load_rq(1, 0)
        load_rq(1, 1)
        wa_raw = staged("wa_raw", [P, PASSES, N // 2], I32, 1024)
        nc.sync.dma_start(out=wa_raw[:], in_=wa_words.rearrange("z p b -> p z b").bitcast(I32))
        load_scale_rows(nc.sync, wa_scales_raw, wa_scales)
        xq_codes = sbuf("xq_codes", [P, PASSES, 2 * T], U8)
        nc.sync.dma_start(out=xq_codes[:].bitcast(I32), in_=xq_words.rearrange("z p b -> p z b").bitcast(I32))
        load_scale_rows(nc.sync, xq_plane, xq_scales)
        gains_t = psum_p.tile([P, P], F32, name="acc_p")
        nc.tensor.transpose(gains_t[:], gain_rows[:], identity[:])
        gains = sbuf("gains", [P, TILES - 1], F32)
        nc.vector.tensor_copy(out=gains[:], in_=gains_t[:, 0 : TILES - 1])
        last_gain = sbuf("last_gain", [P, 1], F32)
        nc.vector.tensor_copy(out=last_gain[:], in_=gains_t[:, TILES - 1 : TILES])

        rq_codes = {}
        rq_plane = [sbuf(f"rq_plane{z}", [P, J], U8) for z in range(PASSES)]
        rq_bf = {}

        def round_rq(h, z):
            woven = sbuf(f"rq_bf{h}{z}", [P, HALF, 4], BF16)
            dst = woven[:].rearrange("p (c i) t -> p c t i", i=4)
            src = rq_raw[h, z][:].rearrange("p t (c i) -> p c t i", i=4)
            if h == 0:
                nc.vector.tensor_copy(out=dst, in_=src)
            else:
                nc.scalar.activation(out=dst, in_=src, func=ACT.Copy)
            rq_bf[h, z] = woven

        def quantise_rq(h, z):
            cols = slice(h * HALF, (h + 1) * HALF)
            name, shape = f"rq_codes{h}{z}", [P, HALF]
            rq_codes[h, z] = staged(name, shape, U32, 1536 + 1024 * z) if h else sbuf(name, shape, U32)
            nc.vector.quantize_mx(
                out=rq_codes[h, z][:].bitcast(FP8X4),
                scales=rq_plane[z][:, cols],
                in_=rq_bf[h, z][:].rearrange("p c t -> p (c t)"),
            )

        for z in range(PASSES):
            round_rq(0, z)
            quantise_rq(0, z)


        wr_plane = sbuf("wr_plane", [P, PASSES, TILES, P], U8)
        wr_codes = [sbuf(f"wr_codes{g}", [P, PASSES, 2, P], I32) for g in range(2)]
        wr_dealt = wr_raw[:].rearrange("p z (u i b) -> p z i u b", i=TILES, b=4)

        def deal_wr(g):
            nc.vector.tensor_copy(
                out=wr_codes[g][:].rearrange("p z i (u b) -> p z i u b", b=4),
                in_=wr_dealt[:, :, 2 * g : 2 * g + 2],
            )

        def deal_scales(plane, raw):
            nc.vector.tensor_copy(
                out=plane[:].bitcast(I32),
                in_=raw[:].bitcast(I32).rearrange("p z (u i) -> p z i u", i=TILES),
            )

        deal_scales(wr_plane, wr_scales_raw)
        deal_wr(0)
        deal_wr(1)

        def patch_product(i, cols):
            acc = psum_p.tile([P, cols.stop - cols.start], F32, name="acc_p")
            for j0 in range(cols.start, cols.stop, HALF):
                for z in range(PASSES):
                    nc.tensor.matmul_mx(
                        out=acc[:, j0 - cols.start : j0 - cols.start + HALF],
                        lhsT=wr_codes[i // 2][:, z, i % 2, :].bitcast(FP8X4),
                        lhsT_scale=wr_plane[:, z, i, :],
                        rhs=rq_codes[j0 // HALF, z][:].bitcast(FP8X4),
                        rhs_scale=rq_plane[z][:, j0 : j0 + HALF],
                        start=(z == 0),
                        stop=(z == PASSES - 1),
                    )
            return acc

        def scale_patches(i, cols, acc, offset):
            name, shape = f"patches{i}_{cols.start}", [P, cols.stop - cols.start]
            patches = sbuf(name, shape, F32) if offset is None else staged(name, shape, F32, offset)
            nc.scalar.activation(out=patches[:], in_=acc[:], func=ACT.Copy, scale=gains[:, i : i + 1] if i + 1 < TILES else last_gain[:])
            return patches

        def place(i, cols, patches):
            entries = offsets[:, cols.start // 16 : cols.stop // 16]
            nc.vector.tensor_copy(pages[i % 2][:].indirect(entries), patches[:])

        first, second, whole = slice(0, HALF), slice(HALF, J), slice(0, J)
        patches_first0 = sbuf("patches_first0", [P, HALF], F32)
        nc.vector.tensor_scalar(
            out=patches_first0[:], in0=patch_product(0, first)[:], scalar1=gains[:, 0:1], scalar2=None, op0=ALU.mult
        )
        place(0, first, patches_first0)
        acc_first1 = patch_product(1, first)
        round_rq(1, 0)
        round_rq(1, 1)

        wa_plane = sbuf("wa_plane", [P, PASSES, TILES, P], U8)
        wa_codes = sbuf("wa_codes", [P, PASSES, TILES, 2 * P], U8, "wa_scales_raw")
        deal_scales(wa_plane, wa_scales_raw)
        nc.vector.tensor_copy(
            out=wa_codes[:].bitcast(I32).rearrange("p z i (u w) -> p z i u w", w=2),
            in_=wa_raw[:].rearrange("p z (u i w) -> p z i u w", i=TILES, w=2),
        )
        for z in range(PASSES):
            quantise_rq(1, z)
        place(1, first, scale_patches(1, first, acc_first1, 512))
        place(0, second, scale_patches(0, second, patch_product(0, second), None))
        place(1, second, scale_patches(1, second, patch_product(1, second), None))

        out_rows = out.rearrange("(u i b) t -> i u b t", i=TILES, b=4)

        def token_product(i, c):
            acc = (psum_p if c < GPSIMD_CHUNKS[i] else psum_v).tile([P, BANK], F32, name="acc_p")
            for z in range(PASSES):
                b0 = c * 2 * BANK
                nc.tensor.matmul_mx(
                    out=acc[:],
                    lhsT=wa_codes[:, z, i, :].bitcast(FP4X4),
                    lhsT_scale=wa_plane[:, z, i, :],
                    rhs=xq_codes[:, z, b0 : b0 + 2 * BANK].bitcast(FP4X4),
                    rhs_scale=xq_plane[:, z, c * BANK : (c + 1) * BANK],
                    start=(z == 0),
                    stop=(z == PASSES - 1),
                )
            if c < GPSIMD_CHUNKS[i]:
                held = sbuf(f"held{i}{c}", [P, BANK], F32)
                nc.scalar.copy(out=held[:], in_=acc[:])
                return held
            return acc

        relu_order = []

        def finish(i, c, sums):
            cols = slice(c * BANK, (c + 1) * BANK)
            name, shape = f"total{i}{c}", [P, BANK]
            total = staged(name, shape, F32, 5120) if (i, c) == (0, 0) else sbuf(name, shape, F32)
            engine = nc.gpsimd if c < GPSIMD_CHUNKS[i] else nc.vector
            engine.tensor_tensor(out=total[:], in0=sums[:], in1=pages[i % 2][:, cols], op=ALU.add)
            on_scalar = (i, c) not in ((3, 0), (3, 3))
            name = f"result{i}{c}"
            if (i, c) in ((0, 1), (0, 2)):
                result = staged(name, shape, F32, 2048 + 2048 * c)
            elif (i, c) == (0, 0):
                result = sbuf(name, shape, F32, "gains")
            else:
                result = sbuf(name, shape, F32, relu_order[-2] if on_scalar else None)
            if on_scalar:
                relu_order.append(f"total{i}{c}")
            if (i, c) == (3, 0):
                engine.tensor_scalar(
                    out=result[:], in0=total[:], scalar1=3.4028234663852886e38, scalar2=0.0, op0=ALU.min, op1=ALU.max
                )
            elif (i, c) == (3, 3):
                engine.tensor_scalar(out=result[:], in0=total[:], scalar1=0.0, scalar2=None, op0=ALU.max)
            else:
                nc.scalar.activation(out=result[:], in_=total[:], func=ACT.Relu)
            nc.sync.dma_start(out=out_rows[i][:, :, cols], in_=result[:])

        sums = {}
        later_patches = {}
        for i in range(TILES):
            for c in range(GPSIMD_CHUNKS[i]):
                sums[i, c] = token_product(i, c)
            if i >= 1:
                for c in range(GPSIMD_CHUNKS[i - 1], CHUNKS):
                    sums[i - 1, c] = token_product(i - 1, c)
            if i + 2 < TILES:
                later_patches[i + 2] = scale_patches(i + 2, whole, patch_product(i + 2, whole), None)
        for i in range(TILES):
            if i >= 2:
                place(i, whole, later_patches[i])
            for c in range(CHUNKS):
                finish(i, c, sums[i, c] if (i, c) in sums else token_product(i, c))
